import numpy as np
import ml_dtypes


def mxq(x, axis, fmt="e4m3"):
    dtype, down = {"e4m3": (ml_dtypes.float8_e4m3fn, 7), "e5m2": (ml_dtypes.float8_e5m2, 14)}[fmt]
    v = np.moveaxis(np.asarray(x, np.float32).astype(ml_dtypes.bfloat16).astype(np.float64), axis, -1)
    blocks = v.reshape(v.shape[:-1] + (-1, 32))
    amax = np.abs(blocks).max(-1, keepdims=True)
    byte = np.maximum(np.where(amax > 0, np.frexp(amax)[1] - 1 + 127, 0) - down, 1)
    scale = np.exp2(byte - 127.0)
    codes = (blocks / scale).astype(np.float32).astype(dtype).astype(np.float64)
    return np.moveaxis((codes * scale).reshape(v.shape), -1, axis)


WIDE = False


def mx_kscale(k):
    if not WIDE:
        return np.ones(k)
    levels = np.array([10, -10, 5, -5, 0])
    if k % 512:
        return np.exp2(np.random.permutation(np.resize(levels, k // 32))).repeat(32)
    a = np.empty((k // 512, 16))
    for p in range(k // 512):
        a[p, :8] = np.random.permutation(np.resize(levels, 8))
        for g in range(8):
            far = levels[np.abs(levels - a[p, g]) >= 10]
            a[p, g + 8] = far[np.random.randint(len(far))]
    return np.exp2(a.ravel()).repeat(32)


def f64(x):
    return np.asarray(x).astype(np.float64)


def striped(idx):
    return np.tile(idx.reshape(-1, 16).T, (8, 1)).astype(np.uint16)


def unstriped(offs):
    return offs[:16].T.reshape(-1).astype(np.int64)


def striped8(idx):
    return np.concatenate([x.reshape(-1, 16).T for x in idx]).astype(np.uint16)


def runs(offs, k):
    lists = np.stack([offs[16 * r : 16 * r + 16].T.reshape(-1) for r in range(8)]).astype(np.int64)
    return lists[np.arange(k) % 512 // 64]


def pack_weight(w):
    k, n = w.shape
    w = f64(np.asarray(w, np.float32).astype(ml_dtypes.bfloat16)).reshape(k // 32, 32, n)
    amax = np.abs(w).max(1)
    byte = np.clip(np.where(amax > 0, np.frexp(amax)[1] - 1 + 127 - 7, 1), 1, 254)
    scaled = (w * np.exp2(127.0 - byte)[:, None, :]).reshape(k, n).astype(np.float32)
    words = np.ascontiguousarray(scaled.reshape(k // 512, 128, 4, n).transpose(0, 1, 3, 2)).astype(ml_dtypes.float8_e4m3fn).view(np.uint8)
    return words, np.ascontiguousarray(byte.astype(np.uint8).reshape(k // 512, 16, n))


def unpack_weight(words, scales):
    g, p, n, _ = words.shape
    vals = np.ascontiguousarray(words).view(ml_dtypes.float8_e4m3fn).astype(np.float64) * np.repeat(np.exp2(scales.astype(np.float64) - 127.0), 8, axis=1)[..., None]
    return vals.transpose(0, 1, 3, 2).reshape(g * 512, n)


def sigmoid(v):
    return 1.0 / (1.0 + np.exp(-np.maximum(v, -700.0)))


K, T, S, N, G, H = 512, 1024, 512, 512, 2048, 512


def setup_inputs():
    n = np.random.standard_normal
    s = mx_kscale(K)[:, None]
    u = mx_kscale(S)
    packed_xT = pack_weight(n((K, T)) * s)
    packed_dT = pack_weight(n((K, G)) / s)
    return {
        "x_words": packed_xT[0],
        "x_scales": packed_xT[1],
        "d_words": packed_dT[0],
        "d_scales": packed_dT[1],
        "gn": (np.random.uniform(0.5, 1.5, (H, 1)) * u[:, None]).astype(np.float32),
        "w1": (n((H, N)) / np.sqrt(H) / u[:, None]).astype(np.float32),
        "offs": striped(np.random.permutation(T)[:S]),
        "k1": striped8(np.random.randint(0, G, (8, H))),
        "two": striped(np.random.permutation(T)[:S]),
        "k2": striped8(np.random.randint(0, G, (8, H))),
        "n1": striped(np.random.permutation(S)),
        "n2": striped(np.random.permutation(S)),
        "n3": striped(np.random.permutation(S)),
        "n4": striped(np.random.permutation(S)),
    }


def reference(x_words, x_scales, d_words, d_scales, gn, w1, offs, k1, two, k2, n1, n2, n3, n4):
    d_k1 = unpack_weight(d_words, d_scales)[np.arange(K)[:, None], runs(k1, K)]
    xq = unpack_weight(x_words, x_scales)[:, unstriped(offs)]
    a = 0.0625 * (d_k1.T @ xq)
    d_k2 = unpack_weight(d_words, d_scales)[np.arange(K)[:, None], runs(k2, K)]
    x_two = unpack_weight(x_words, x_scales)[:, unstriped(two)]
    b = 0.0625 * (d_k2.T @ x_two)
    z = f64(gn) * (a + (sigmoid(b[:, unstriped(n2)] - b)) * (a[:, unstriped(n1)] - a))
    h = mxq(f64(w1), 0, "e4m3").T @ mxq(z, 0, "e4m3")
    return h[:, unstriped(n3)] / (np.abs(h) + np.abs(h[:, unstriped(n4)]) + 0.5)

@@ -1,0 +1,204 @@
+from contextlib import ExitStack
+
+import concourse.mybir as mybir
+
+F32 = mybir.dt.float32
+BF16 = mybir.dt.bfloat16
+I32 = mybir.dt.int32
+U32 = mybir.dt.uint32
+U16 = mybir.dt.uint16
+U8 = mybir.dt.uint8
+FP8X4 = mybir.dt.float8_e4m3fn_x4
+ALU = mybir.AluOpType
+ACT = mybir.ActivationFunctionType
+
+P = 128
+K, T, S, N, G, H = 512, 1024, 512, 512, 2048, 512
+SPARE = 16
+HALF = S // 2
+FLOPS = 3 * 2 * 512 * 512 * 512
+
+B_ON_SCALAR = [0,1,2,3]
+A_ON_SCALAR = []
+
+
+def tile_picked_twpqpullbnorm2_none_p_kernel(
+    tc, x_words, x_scales, d_words, d_scales, gn, w1, offs, k1, two, k2, n1, n2, n3, n4, out
+):
+    nc = tc.nc
+    with ExitStack() as ctx:
+        lists = ctx.enter_context(tc.tile_pool(name="lists", bufs=1))
+        keep = ctx.enter_context(tc.tile_pool(name="keep", bufs=1))
+        psum = ctx.enter_context(tc.psum_pool(name="psum", bufs=1))
+
+        def load_list(src, name):
+            t = lists.tile([P, S // 16], U16, name=name)
+            nc.sync.dma_start(t[:], src)
+            return t
+
+        d_bytes = keep.tile([P, G], U8, name="d_bytes")
+        x_bytes = keep.tile([P, T], U8, name="x_bytes")
+        nc.gpsimd.memset(d_bytes[:].bitcast(I32), 0)
+        nc.vector.memset(x_bytes[:].bitcast(I32), 0)
+        nc.sync.dma_start(d_bytes[0:P:8, :].bitcast(I32), d_scales[0].bitcast(I32))
+        k2_t = load_list(k2, "k2_t")
+        nc.sync.dma_start(x_bytes[0:P:8, :].bitcast(I32), x_scales[0].bitcast(I32))
+        two_t = load_list(two, "two_t")
+        x_tab = keep.tile([P, T], U32, name="x_tab")
+        nc.sync.dma_start(x_tab[:].bitcast(I32), x_words[0].rearrange("p n t -> p (n t)").bitcast(I32))
+        d_tab = keep.tile([P, G], U32, name="d_tab")
+        nc.sync.dma_start(d_tab[:].bitcast(I32), d_words[0].rearrange("p n t -> p (n t)").bitcast(I32))
+        k1_t = load_list(k1, "k1_t")
+        offs_t = load_list(offs, "offs_t")
+        n2_t = load_list(n2, "n2_t")
+        n1_t = load_list(n1, "n1_t")
+        w_raw = [keep.tile([P, 4, N // 2], F32, name="w_raw%d" % c) for c in range(2)]
+        for c in range(2):
+            nc.sync.dma_start(w_raw[c][:], w1[:, c * 256:(c + 1) * 256].rearrange("(p j) n -> p j n", j=4))
+        gain = keep.tile([P, 4], F32, name="gain")
+        nc.gpsimd.dma_start(gain[:], gn.rearrange("(p t) o -> p (t o)", t=4))
+        n4_t = load_list(n4, "n4_t")
+        n3_t = load_list(n3, "n3_t")
+
+        planes = [keep.tile([P, 2 * S], U8, name="planes%d" % i, align_bytes=64) for i in range(2)]
+        for t in planes:
+            nc.gpsimd.memset(t[:].bitcast(I32), 0)
+        b_win = [keep.tile([P, S + SPARE], F32, name="b_win%d" % t) for t in range(4)]
+        a_win = [keep.tile([P, S + SPARE], F32, name="a_win%d" % t) for t in range(4) if t not in A_ON_SCALAR]
+        h_win = [keep.tile([P, S + SPARE], F32, name="h_win%d" % t) for t in range(4)]
+        m_win = [keep.tile([P, S + SPARE], F32, name="m_win%d" % t) for t in range(4)]
+        for t in b_win + a_win + h_win + m_win:
+            nc.gpsimd.memset(t[:, S:], 0.0)
+        g_pos = [keep.tile([P, 1], F32, name="g_pos%d" % t, tag="gate%d" % t) for t in range(4)]
+        g_neg = keep.tile([P, 4], F32, name="g_neg")
+        for t in range(4):
+            nc.gpsimd.tensor_scalar(g_pos[t][:], gain[:, t:t + 1], 0.0625, 0.0, ALU.mult, ALU.add)
+        nc.gpsimd.tensor_scalar(g_neg[:], gain[:], -0.0625, 0.0, ALU.mult, ALU.add)
+
+        def coded_layer(code_list, token_list, plane, name, tags, queue):
+            got = keep.tile([P, 2 * S], U8, name=name + "_got", tag=tags[0], align_bytes=64)
+            nc.vector.tensor_copy(got[:, :H], d_bytes[:].indirect(code_list[:]))
+            nc.vector.tensor_copy(got[:, H:], x_bytes[:].indirect(token_list[:]))
+            dealt = keep.tile([P, 2 * S], U8, name=name + "_dealt")
+            nc.vector.tensor_copy(
+                dealt[:, :H].rearrange("p (t c i) -> p c t i", t=4, i=16),
+                got[:, :H].rearrange("p (c i t) -> p c t i", t=4, i=16),
+            )
+            nc.vector.tensor_copy(dealt[:, H:].bitcast(I32), got[:, H:].bitcast(I32))
+            for i in range(4):
+                queue.dma_start(plane[i:P:32, :].bitcast(I32), dealt[8 * i:P:32, :].bitcast(I32))
+            xq = keep.tile([P, S], U32, name=name + "_xq", tag=tags[1], align_bytes=64)
+            nc.vector.tensor_copy(xq[:], x_tab[:].indirect(token_list[:]))
+            dq = keep.tile([P, H], U32, name=name + "_dq", tag=tags[2], align_bytes=64)
+            nc.vector.tensor_copy(dq[:], d_tab[:].indirect(code_list[:]))
+            dd = keep.tile([P, H], U32, name=name + "_dd", align_bytes=64)
+            nc.vector.tensor_copy(
+                dd[:].rearrange("p (t c i) -> p c t i", t=4, i=4),
+                dq[:].rearrange("p (c i t) -> p c t i", t=4, i=4),
+            )
+            banks = []
+            for t in range(4):
+                acc = psum.tile([P, S], F32, name="%s_acc%d" % (name, t), tag="bank_%s%d" % (name, t))
+                cols = slice(t * P, (t + 1) * P)
+                nc.tensor.matmul_mx(
+                    acc[:], lhsT=dd[:, cols].bitcast(FP8X4), lhsT_scale=plane[:, cols],
+                    rhs=xq[:].bitcast(FP8X4), rhs_scale=plane[:, H:], start=True, stop=True,
+                )
+                banks.append(acc)
+            return banks
+
+        w_bf = keep.tile([P, N, 4], BF16, name="w_bf", align_bytes=64)
+        for c in range(2):
+            nc.scalar.copy(
+                w_bf[:, c * 256:(c + 1) * 256, :].rearrange("p (c i) t -> p c t i", i=2),
+                w_raw[c][:].rearrange("p t (c i) -> p c t i", i=2),
+            )
+
+        b_acc = coded_layer(k2_t, two_t, planes[0], "b", ("b_got", "b_xq", "chain"), nc.sync)
+        a_acc = coded_layer(k1_t, offs_t, planes[1], "a", ("chain", "chain", "a_dq"), nc.sync)
+
+        w_codes = keep.tile([P, N], U32, name="w_codes", align_bytes=64)
+        w_plane = keep.tile([P, N], U8, name="w_plane", align_bytes=64)
+        nc.vector.quantize_mx(w_codes[:].bitcast(FP8X4), w_plane[:], w_bf[:].rearrange("p n t -> p (n t)"))
+
+        db = []
+        for t in range(4):
+            nc.scalar.copy(b_win[t][:, :S], b_acc[t][:])
+            d_t = keep.tile([P, S], F32, name="db%d" % t)
+            o_t = keep.tile([P, S], F32, name="bo%d" % t)
+            if t in B_ON_SCALAR:
+                nc.scalar.activation(o_t[:], b_win[t][:].indirect(n2_t[:]), ACT.Copy)
+                nc.vector.tensor_tensor(d_t[:], o_t[:], b_acc[t][:], ALU.subtract)
+            else:
+                nc.vector.tensor_scalar(o_t[:], b_win[t][:, :S], -1.0, None, ALU.mult)
+                nc.vector.tensor_tensor(d_t[:], b_win[t][:].indirect(n2_t[:]), o_t[:], ALU.add)
+            db.append(d_t)
+
+        a_neg = keep.tile([P, 4, S], F32, name="a_neg")
+        pull = keep.tile([P, 4, S], F32, name="pull")
+        da = [keep.tile([P, S], F32, name="da%d" % t) for t in range(4)]
+        sg = []
+
+        def pull_cols(t, lo, hi):
+            nc.vector.tensor_tensor(da[t][:, lo:hi], a_win[t][:].indirect(n1_t[:, lo // 16:hi // 16]), a_neg[:, t, lo:hi], ALU.add)
+            nc.vector.tensor_tensor(pull[:, t, lo:hi], sg[t][:, lo:hi], da[t][:, lo:hi], ALU.mult)
+
+        for t in range(4):
+            nc.scalar.activation(a_neg[:, t, :], a_acc[t][:], ACT.Copy, scale=g_neg[:, t:t + 1])
+            nc.scalar.activation(a_win[t][:, :S], a_acc[t][:], ACT.Copy, scale=g_pos[t][:])
+            sg.append(keep.tile([P, S], F32, name="sg%d" % t, tag="gate%d" % t))
+            nc.scalar.activation(sg[t][:], db[t][:], ACT.Sigmoid, scale=0.0625)
+            if t < 3:
+                pull_cols(t, 0, S)
+
+        z_codes = keep.tile([P, S], U32, name="z_codes", align_bytes=64)
+        z_plane = keep.tile([P, S], U8, name="z_plane", align_bytes=64)
+        z_bf = [keep.tile([P, HALF, 4], BF16, name="z_bf%d" % c, align_bytes=64) for c in range(2)]
+        h_acc = []
+        for c in range(2):
+            cols = slice(c * HALF, (c + 1) * HALF)
+            pull_cols(3, c * HALF, (c + 1) * HALF)
+            nc.vector.tensor_tensor(
+                z_bf[c][:].rearrange("p (c i) t -> p c t i", i=2),
+                pull[:, :, cols].rearrange("p t (c i) -> p c t i", i=2),
+                a_neg[:, :, cols].rearrange("p t (c i) -> p c t i", i=2),
+                ALU.subtract,
+            )
+            nc.vector.quantize_mx(z_codes[:, cols].bitcast(FP8X4), z_plane[:, cols], z_bf[c][:].rearrange("p n t -> p (n t)"))
+            row = []
+            for t in range(4):
+                acc = psum.tile([P, HALF], F32, name="h_acc%d%d" % (c, t), tag="bank_%s%d" % ("ba"[c], t))
+                rows = slice(t * P, (t + 1) * P)
+                nc.tensor.matmul_mx(
+                    acc[:], lhsT=w_codes[:, rows].bitcast(FP8X4), lhsT_scale=w_plane[:, rows],
+                    rhs=z_codes[:, cols].bitcast(FP8X4), rhs_scale=z_plane[:, cols], start=True, stop=True,
+                )
+                row.append(acc)
+            h_acc.append(row)
+
+        mag = [keep.tile([P, S], F32, name="mag%d" % t) for t in range(4)]
+        for t in range(4):
+            nc.scalar.activation(m_win[t][:, :HALF], h_acc[0][t][:], ACT.Abs)
+        for t in range(4):
+            nc.scalar.copy(h_win[t][:, :HALF], h_acc[0][t][:])
+            nc.vector.tensor_copy(mag[t][:, :HALF], m_win[t][:, :HALF])
+        for t in range(4):
+            nc.scalar.activation(m_win[t][:, HALF:S], h_acc[1][t][:], ACT.Abs)
+            if t == 0:
+                nc.vector.tensor_copy(mag[t][:, HALF:], m_win[t][:, HALF:S])
+            else:
+                nc.scalar.activation(mag[t][:, HALF:], h_acc[1][t][:], ACT.Abs)
+        den = [keep.tile([P, S], F32, name="den%d" % t) for t in range(4)]
+        for t in range(4):
+            nc.vector.tensor_tensor(den[t][:], m_win[t][:].indirect(n4_t[:]), mag[t][:], ALU.add)
+        r = []
+        for t in range(4):
+            q = keep.tile([P, S], F32, name="q%d" % t)
+            nc.scalar.activation(q[:], den[t][:], ACT.Abs_reciprocal_sqrt, bias=0.5)
+            r.append(keep.tile([P, S], F32, name="r%d" % t))
+            nc.scalar.activation(r[t][:], q[:], ACT.Square)
+            nc.scalar.copy(h_win[t][:, HALF:S], h_acc[1][t][:])
+        for t in range(4):
+            o = keep.tile([P, S], F32, name="o%d" % t)
+            nc.vector.tensor_tensor(o[:], h_win[t][:].indirect(n3_t[:]), r[t][:], ALU.mult)
+            nc.sync.dma_start(out[t * P:(t + 1) * P, :], o[:])

@@ -36,6 +36,7 @@ def tile_picked_twpqpullbnorm2_none_p_kernel(
             nc.sync.dma_start(t[:], src)
             return t
 
+        warm = keep.tile([P, 3, 8], F32, name="warm")
         d_bytes = keep.tile([P, G], U8, name="d_bytes")
         x_bytes = keep.tile([P, T], U8, name="x_bytes")
         nc.gpsimd.memset(d_bytes[:].bitcast(I32), 0)
@@ -60,6 +61,8 @@ def tile_picked_twpqpullbnorm2_none_p_kernel(
         n4_t = load_list(n4, "n4_t")
         n3_t = load_list(n3, "n3_t")
 
+        nc.vector.memset(warm[:, 0, :], 1.0)
+        nc.scalar.activation(warm[:, 1, :], warm[:, 0, :], ACT.Sigmoid)
         planes = [keep.tile([P, 2 * S], U8, name="planes%d" % i, align_bytes=64) for i in range(2)]
         for t in planes:
             nc.gpsimd.memset(t[:].bitcast(I32), 0)
@@ -151,6 +154,7 @@ def tile_picked_twpqpullbnorm2_none_p_kernel(
             if t < 3:
                 pull_cols(t, 0, S)
 
+        nc.scalar.activation(warm[:, 2, :], sg[3][:, :8], ACT.Abs_reciprocal_sqrt, bias=0.5)
         z_codes = keep.tile([P, S], U32, name="z_codes", align_bytes=64)
         z_plane = keep.tile([P, S], U8, name="z_plane", align_bytes=64)
         z_bf = [keep.tile([P, HALF, 4], BF16, name="z_bf%d" % c, align_bytes=64) for c in range(2)]

@@ -18,8 +18,9 @@ SPARE = 16
 HALF = S // 2
 FLOPS = 3 * 2 * 512 * 512 * 512
 
-B_ON_SCALAR = [0,1,2,3]
-A_ON_SCALAR = []
+B_ON_VECTOR = [0]
+SPLIT = [2,3]
+MAG_ON_VECTOR = []
 
 
 def tile_picked_twpqpullbnorm2_none_p_kernel(
@@ -43,31 +44,28 @@ def tile_picked_twpqpullbnorm2_none_p_kernel(
         nc.vector.memset(x_bytes[:].bitcast(I32), 0)
         nc.sync.dma_start(d_bytes[0:P:8, :].bitcast(I32), d_scales[0].bitcast(I32))
         k2_t = load_list(k2, "k2_t")
-        nc.sync.dma_start(x_bytes[0:P:8, :].bitcast(I32), x_scales[0].bitcast(I32))
         two_t = load_list(two, "two_t")
         x_tab = keep.tile([P, T], U32, name="x_tab")
         nc.sync.dma_start(x_tab[:].bitcast(I32), x_words[0].rearrange("p n t -> p (n t)").bitcast(I32))
-        d_tab = keep.tile([P, G], U32, name="d_tab")
-        nc.sync.dma_start(d_tab[:].bitcast(I32), d_words[0].rearrange("p n t -> p (n t)").bitcast(I32))
+        nc.sync.dma_start(x_bytes[0:P:8, :].bitcast(I32), x_scales[0].bitcast(I32))
         k1_t = load_list(k1, "k1_t")
         offs_t = load_list(offs, "offs_t")
+        d_tab = keep.tile([P, G], U32, name="d_tab")
+        nc.sync.dma_start(d_tab[:].bitcast(I32), d_words[0].rearrange("p n t -> p (n t)").bitcast(I32))
+        w_raw = [keep.tile([P, 4, N // 2], F32, name="w_raw%d" % c) for c in range(2)]
+
+        def load_w(c):
+            nc.sync.dma_start(w_raw[c][:], w1[:, c * 256:(c + 1) * 256].rearrange("(p j) n -> p j n", j=4))
+
+        load_w(0)
         n2_t = load_list(n2, "n2_t")
         n1_t = load_list(n1, "n1_t")
-        w_raw = [keep.tile([P, 4, N // 2], F32, name="w_raw%d" % c) for c in range(2)]
-        for c in range(2):
-            nc.sync.dma_start(w_raw[c][:], w1[:, c * 256:(c + 1) * 256].rearrange("(p j) n -> p j n", j=4))
         gain = keep.tile([P, 4], F32, name="gain")
         nc.gpsimd.dma_start(gain[:], gn.rearrange("(p t) o -> p (t o)", t=4))
-        n4_t = load_list(n4, "n4_t")
-        n3_t = load_list(n3, "n3_t")
-
         nc.vector.memset(warm[:, 0, :], 1.0)
         nc.scalar.activation(warm[:, 1, :], warm[:, 0, :], ACT.Sigmoid)
-        planes = [keep.tile([P, 2 * S], U8, name="planes%d" % i, align_bytes=64) for i in range(2)]
-        for t in planes:
-            nc.gpsimd.memset(t[:].bitcast(I32), 0)
         b_win = [keep.tile([P, S + SPARE], F32, name="b_win%d" % t) for t in range(4)]
-        a_win = [keep.tile([P, S + SPARE], F32, name="a_win%d" % t) for t in range(4) if t not in A_ON_SCALAR]
+        a_win = [keep.tile([P, S + SPARE], F32, name="a_win%d" % t) for t in range(3)]
         h_win = [keep.tile([P, S + SPARE], F32, name="h_win%d" % t) for t in range(4)]
         m_win = [keep.tile([P, S + SPARE], F32, name="m_win%d" % t) for t in range(4)]
         for t in b_win + a_win + h_win + m_win:
@@ -75,25 +73,32 @@ def tile_picked_twpqpullbnorm2_none_p_kernel(
         g_pos = [keep.tile([P, 1], F32, name="g_pos%d" % t, tag="gate%d" % t) for t in range(4)]
         g_neg = keep.tile([P, 4], F32, name="g_neg")
         for t in range(4):
-            nc.gpsimd.tensor_scalar(g_pos[t][:], gain[:, t:t + 1], 0.0625, 0.0, ALU.mult, ALU.add)
+            nc.gpsimd.tensor_scalar(g_pos[t][:], gain[:, t:t + 1], 0.0625 if t < 3 else -0.0625, 0.0, ALU.mult, ALU.add)
         nc.gpsimd.tensor_scalar(g_neg[:], gain[:], -0.0625, 0.0, ALU.mult, ALU.add)
 
-        def coded_layer(code_list, token_list, plane, name, tags, queue):
+        def coded_layer(code_list, token_list, name, tags):
             got = keep.tile([P, 2 * S], U8, name=name + "_got", tag=tags[0], align_bytes=64)
             nc.vector.tensor_copy(got[:, :H], d_bytes[:].indirect(code_list[:]))
             nc.vector.tensor_copy(got[:, H:], x_bytes[:].indirect(token_list[:]))
-            dealt = keep.tile([P, 2 * S], U8, name=name + "_dealt")
+            dealt = keep.tile([P, 2 * S], U8, name=name + "_dealt", tag=tags[3], align_bytes=64)
             nc.vector.tensor_copy(
                 dealt[:, :H].rearrange("p (t c i) -> p c t i", t=4, i=16),
                 got[:, :H].rearrange("p (c i t) -> p c t i", t=4, i=16),
             )
             nc.vector.tensor_copy(dealt[:, H:].bitcast(I32), got[:, H:].bitcast(I32))
-            for i in range(4):
-                queue.dma_start(plane[i:P:32, :].bitcast(I32), dealt[8 * i:P:32, :].bitcast(I32))
-            xq = keep.tile([P, S], U32, name=name + "_xq", tag=tags[1], align_bytes=64)
-            nc.vector.tensor_copy(xq[:], x_tab[:].indirect(token_list[:]))
-            dq = keep.tile([P, H], U32, name=name + "_dq", tag=tags[2], align_bytes=64)
-            nc.vector.tensor_copy(dq[:], d_tab[:].indirect(code_list[:]))
+            plane = dealt
+            for i in range(1, 4):
+                nc.sync.dma_start(plane[i:P:32, :].bitcast(I32), dealt[8 * i:P:32, :].bitcast(I32))
+            if name == "b":
+                xq = keep.tile([P, S], U32, name="b_xq", align_bytes=64)
+                nc.vector.tensor_copy(xq[:], x_tab[:].indirect(token_list[:]))
+                dq = keep.tile([P, H], U32, name="b_dq", tag="chain", align_bytes=64)
+                nc.vector.tensor_copy(dq[:], d_tab[:].indirect(code_list[:]))
+            else:
+                both = keep.tile([P, H + S], U32, name="a_words", tag="chain", align_bytes=64)
+                dq, xq = both[:, :H], both[:, H:]
+                nc.vector.tensor_copy(dq, d_tab[:].indirect(code_list[:]))
+                nc.vector.tensor_copy(xq, x_tab[:].indirect(token_list[:]))
             dd = keep.tile([P, H], U32, name=name + "_dd", align_bytes=64)
             nc.vector.tensor_copy(
                 dd[:].rearrange("p (t c i) -> p c t i", t=4, i=4),
@@ -110,64 +115,82 @@ def tile_picked_twpqpullbnorm2_none_p_kernel(
                 banks.append(acc)
             return banks
 
-        w_bf = keep.tile([P, N, 4], BF16, name="w_bf", align_bytes=64)
-        for c in range(2):
+        w_codes = keep.tile([P, N], U32, name="w_codes", align_bytes=64)
+        w_plane = keep.tile([P, N], U8, name="w_plane", align_bytes=64)
+        w_bf = []
+
+        def round_w(c, tag):
+            w_bf.append(keep.tile([P, N // 2, 4], BF16, name="w_bf%d" % c, tag=tag, align_bytes=64))
             nc.scalar.copy(
-                w_bf[:, c * 256:(c + 1) * 256, :].rearrange("p (c i) t -> p c t i", i=2),
+                w_bf[c][:].rearrange("p (c i) t -> p c t i", i=2),
                 w_raw[c][:].rearrange("p t (c i) -> p c t i", i=2),
             )
 
-        b_acc = coded_layer(k2_t, two_t, planes[0], "b", ("b_got", "b_xq", "chain"), nc.sync)
-        a_acc = coded_layer(k1_t, offs_t, planes[1], "a", ("chain", "chain", "a_dq"), nc.sync)
+        def quantize_w(c):
+            cols = slice(c * 256, (c + 1) * 256)
+            nc.vector.quantize_mx(w_codes[:, cols].bitcast(FP8X4), w_plane[:, cols], w_bf[c][:].rearrange("p n t -> p (n t)"))
 
-        w_codes = keep.tile([P, N], U32, name="w_codes", align_bytes=64)
-        w_plane = keep.tile([P, N], U8, name="w_plane", align_bytes=64)
-        nc.vector.quantize_mx(w_codes[:].bitcast(FP8X4), w_plane[:], w_bf[:].rearrange("p n t -> p (n t)"))
+        round_w(0, "w_bf0")
+        b_acc = coded_layer(k2_t, two_t, "b", ("b_got", "b_xq", "chain", "b_dealt"))
+        n4_t = load_list(n4, "n4_t")
+        n3_t = load_list(n3, "n3_t")
+        load_w(1)
+        a_acc = coded_layer(k1_t, offs_t, "a", ("chain", "chain", "a_dq", "a_dealt"))
 
-        db = []
+        db = [keep.tile([P, S], F32, name="db%d" % t, tag="db%d" % t, align_bytes=64) for t in range(4)]
+        other = [keep.tile([P, S], F32, name="bo%d" % t) for t in range(4)]
         for t in range(4):
             nc.scalar.copy(b_win[t][:, :S], b_acc[t][:])
-            d_t = keep.tile([P, S], F32, name="db%d" % t)
-            o_t = keep.tile([P, S], F32, name="bo%d" % t)
-            if t in B_ON_SCALAR:
-                nc.scalar.activation(o_t[:], b_win[t][:].indirect(n2_t[:]), ACT.Copy)
-                nc.vector.tensor_tensor(d_t[:], o_t[:], b_acc[t][:], ALU.subtract)
-            else:
-                nc.vector.tensor_scalar(o_t[:], b_win[t][:, :S], -1.0, None, ALU.mult)
-                nc.vector.tensor_tensor(d_t[:], b_win[t][:].indirect(n2_t[:]), o_t[:], ALU.add)
-            db.append(d_t)
+            if t > 0:
+                nc.scalar.activation(other[t][:], b_win[t][:].indirect(n2_t[:]), ACT.Copy)
+        nc.vector.tensor_scalar(other[0][:], b_win[0][:, :S], -1.0, None, ALU.mult)
+        quantize_w(0)
+        nc.vector.tensor_tensor(db[0][:], b_win[0][:].indirect(n2_t[:]), other[0][:], ALU.add)
+        for t in range(1, 4):
+            nc.vector.tensor_tensor(db[t][:], other[t][:], b_acc[t][:], ALU.subtract)
 
         a_neg = keep.tile([P, 4, S], F32, name="a_neg")
         pull = keep.tile([P, 4, S], F32, name="pull")
         da = [keep.tile([P, S], F32, name="da%d" % t) for t in range(4)]
         sg = []
+        whole, first, second = (0, S), (0, HALF), (HALF, S)
 
-        def pull_cols(t, lo, hi):
-            nc.vector.tensor_tensor(da[t][:, lo:hi], a_win[t][:].indirect(n1_t[:, lo // 16:hi // 16]), a_neg[:, t, lo:hi], ALU.add)
-            nc.vector.tensor_tensor(pull[:, t, lo:hi], sg[t][:, lo:hi], da[t][:, lo:hi], ALU.mult)
-
-        for t in range(4):
+        def leave_bank(t):
             nc.scalar.activation(a_neg[:, t, :], a_acc[t][:], ACT.Copy, scale=g_neg[:, t:t + 1])
             nc.scalar.activation(a_win[t][:, :S], a_acc[t][:], ACT.Copy, scale=g_pos[t][:])
             sg.append(keep.tile([P, S], F32, name="sg%d" % t, tag="gate%d" % t))
-            nc.scalar.activation(sg[t][:], db[t][:], ACT.Sigmoid, scale=0.0625)
-            if t < 3:
-                pull_cols(t, 0, S)
 
-        nc.scalar.activation(warm[:, 2, :], sg[3][:, :8], ACT.Abs_reciprocal_sqrt, bias=0.5)
+        def gate(t, span):
+            lo, hi = span
+            nc.scalar.activation(sg[t][:, lo:hi], db[t][:, lo:hi], ACT.Sigmoid, scale=0.0625)
+
+        def diff(t, span):
+            lo, hi = span
+            if t == 3:
+                nc.vector.scalar_tensor_tensor(da[t][:, lo:hi], a_acc[t][:, lo:hi], g_neg[:, t:t + 1], fetched[:, lo:hi], ALU.mult, ALU.subtract)
+                return
+            nc.vector.tensor_tensor(da[t][:, lo:hi], a_win[t][:].indirect(n1_t[:, lo // 16:hi // 16]), a_neg[:, t, lo:hi], ALU.add)
+
+        def weigh(t, span):
+            lo, hi = span
+            nc.vector.tensor_tensor(pull[:, t, lo:hi], sg[t][:, lo:hi], da[t][:, lo:hi], ALU.mult)
+
         z_codes = keep.tile([P, S], U32, name="z_codes", align_bytes=64)
         z_plane = keep.tile([P, S], U8, name="z_plane", align_bytes=64)
         z_bf = [keep.tile([P, HALF, 4], BF16, name="z_bf%d" % c, align_bytes=64) for c in range(2)]
         h_acc = []
-        for c in range(2):
+
+        def blend(c):
             cols = slice(c * HALF, (c + 1) * HALF)
-            pull_cols(3, c * HALF, (c + 1) * HALF)
             nc.vector.tensor_tensor(
                 z_bf[c][:].rearrange("p (c i) t -> p c t i", i=2),
                 pull[:, :, cols].rearrange("p t (c i) -> p c t i", i=2),
                 a_neg[:, :, cols].rearrange("p t (c i) -> p c t i", i=2),
                 ALU.subtract,
             )
+
+        def dense(c):
+            cols = slice(c * HALF, (c + 1) * HALF)
             nc.vector.quantize_mx(z_codes[:, cols].bitcast(FP8X4), z_plane[:, cols], z_bf[c][:].rearrange("p n t -> p (n t)"))
             row = []
             for t in range(4):
@@ -180,21 +203,56 @@ def tile_picked_twpqpullbnorm2_none_p_kernel(
                 row.append(acc)
             h_acc.append(row)
 
+        leave_bank(0)
+        leave_bank(1)
+        gate(0, whole)
+        leave_bank(2)
+        gate(1, whole)
+        nc.scalar.activation(a_neg[:, 3, :], a_acc[3][:], ACT.Copy, scale=g_pos[3][:])
+        sg.append(keep.tile([P, S], F32, name="sg3", tag="gate3"))
+        fetched = keep.tile([P, S], F32, name="fetched")
+        nc.scalar.activation(fetched[:, :HALF], a_neg[:, 3, :].indirect(n1_t[:, :16]), ACT.Copy)
+        gate(2, first)
+        gate(3, first)
+        nc.scalar.activation(fetched[:, HALF:], a_neg[:, 3, :].indirect(n1_t[:, 16:]), ACT.Copy)
+        gate(2, second)
+        gate(3, second)
+        round_w(1, "db3")
+        nc.scalar.activation(warm[:, 2, :], sg[3][:, S - 8:], ACT.Abs_reciprocal_sqrt, bias=0.5)
+
+        diff(0, whole)
+        diff(1, whole)
+        weigh(0, whole)
+        diff(2, first)
+        weigh(1, whole)
+        diff(3, first)
+        weigh(2, first)
+        weigh(3, first)
+        diff(2, second)
+        blend(0)
+        diff(3, second)
+        quantize_w(1)
+        dense(0)
+        weigh(2, second)
+        weigh(3, second)
+        blend(1)
         mag = [keep.tile([P, S], F32, name="mag%d" % t) for t in range(4)]
         for t in range(4):
             nc.scalar.activation(m_win[t][:, :HALF], h_acc[0][t][:], ACT.Abs)
-        for t in range(4):
-            nc.scalar.copy(h_win[t][:, :HALF], h_acc[0][t][:])
             nc.vector.tensor_copy(mag[t][:, :HALF], m_win[t][:, :HALF])
+            if t == 0:
+                dense(1)
         for t in range(4):
             nc.scalar.activation(m_win[t][:, HALF:S], h_acc[1][t][:], ACT.Abs)
-            if t == 0:
+            if t in MAG_ON_VECTOR:
                 nc.vector.tensor_copy(mag[t][:, HALF:], m_win[t][:, HALF:S])
             else:
                 nc.scalar.activation(mag[t][:, HALF:], h_acc[1][t][:], ACT.Abs)
         den = [keep.tile([P, S], F32, name="den%d" % t) for t in range(4)]
         for t in range(4):
             nc.vector.tensor_tensor(den[t][:], m_win[t][:].indirect(n4_t[:]), mag[t][:], ALU.add)
+        for t in range(4):
+            nc.scalar.copy(h_win[t][:, :HALF], h_acc[0][t][:])
         r = []
         for t in range(4):
             q = keep.tile([P, S], F32, name="q%d" % t)
@@ -204,5 +262,6 @@ def tile_picked_twpqpullbnorm2_none_p_kernel(
             nc.scalar.copy(h_win[t][:, HALF:S], h_acc[1][t][:])
         for t in range(4):
             o = keep.tile([P, S], F32, name="o%d" % t)
-            nc.vector.tensor_tensor(o[:], h_win[t][:].indirect(n3_t[:]), r[t][:], ALU.mult)
-            nc.sync.dma_start(out[t * P:(t + 1) * P, :], o[:])
+            for lo, hi in ([(0, S)] if t < 3 else [(0, HALF), (HALF, S)]):
+                nc.vector.tensor_tensor(o[:, lo:hi], h_win[t][:].indirect(n3_t[:, lo // 16:hi // 16]), r[t][:, lo:hi], ALU.mult)
+                nc.sync.dma_start(out[t * P:(t + 1) * P, lo:hi], o[:, lo:hi])

@@ -30,6 +30,7 @@ def tile_picked_twpqpullbnorm2_none_p_kernel(
     with ExitStack() as ctx:
         lists = ctx.enter_context(tc.tile_pool(name="lists", bufs=1))
         keep = ctx.enter_context(tc.tile_pool(name="keep", bufs=1))
+        relay = ctx.enter_context(tc.tile_pool(name="relay", bufs=1))
         psum = ctx.enter_context(tc.psum_pool(name="psum", bufs=1))
 
         def load_list(src, name):
@@ -47,19 +48,19 @@ def tile_picked_twpqpullbnorm2_none_p_kernel(
         two_t = load_list(two, "two_t")
         x_tab = keep.tile([P, T], U32, name="x_tab")
         nc.sync.dma_start(x_tab[:].bitcast(I32), x_words[0].rearrange("p n t -> p (n t)").bitcast(I32))
-        nc.sync.dma_start(x_bytes[0:P:8, :].bitcast(I32), x_scales[0].bitcast(I32))
-        k1_t = load_list(k1, "k1_t")
-        offs_t = load_list(offs, "offs_t")
+        for i in range(4):
+            nc.sync.dma_start(x_bytes[i:P:32, :].bitcast(I32), x_scales[0, i:16:4, :].bitcast(I32))
         d_tab = keep.tile([P, G], U32, name="d_tab")
         nc.sync.dma_start(d_tab[:].bitcast(I32), d_words[0].rearrange("p n t -> p (n t)").bitcast(I32))
+        k1_t = load_list(k1, "k1_t")
+        offs_t = load_list(offs, "offs_t")
         w_raw = [keep.tile([P, 4, N // 2], F32, name="w_raw%d" % c) for c in range(2)]
 
         def load_w(c):
             nc.sync.dma_start(w_raw[c][:], w1[:, c * 256:(c + 1) * 256].rearrange("(p j) n -> p j n", j=4))
 
-        load_w(0)
         n2_t = load_list(n2, "n2_t")
-        n1_t = load_list(n1, "n1_t")
+        load_w(0)
         gain = keep.tile([P, 4], F32, name="gain")
         nc.gpsimd.dma_start(gain[:], gn.rearrange("(p t) o -> p (t o)", t=4))
         nc.vector.memset(warm[:, 0, :], 1.0)
@@ -73,29 +74,37 @@ def tile_picked_twpqpullbnorm2_none_p_kernel(
         g_pos = [keep.tile([P, 1], F32, name="g_pos%d" % t, tag="gate%d" % t) for t in range(4)]
         g_neg = keep.tile([P, 4], F32, name="g_neg")
         for t in range(4):
-            nc.gpsimd.tensor_scalar(g_pos[t][:], gain[:, t:t + 1], 0.0625 if t < 3 else -0.0625, 0.0, ALU.mult, ALU.add)
+            nc.gpsimd.tensor_scalar(g_pos[t][:], gain[:, t:t + 1], 0.0625 if t in (1, 2) else -0.0625, 0.0, ALU.mult, ALU.add)
         nc.gpsimd.tensor_scalar(g_neg[:], gain[:], -0.0625, 0.0, ALU.mult, ALU.add)
 
-        def coded_layer(code_list, token_list, name, tags):
-            got = keep.tile([P, 2 * S], U8, name=name + "_got", tag=tags[0], align_bytes=64)
-            nc.vector.tensor_copy(got[:, :H], d_bytes[:].indirect(code_list[:]))
-            nc.vector.tensor_copy(got[:, H:], x_bytes[:].indirect(token_list[:]))
-            dealt = keep.tile([P, 2 * S], U8, name=name + "_dealt", tag=tags[3], align_bytes=64)
-            nc.vector.tensor_copy(
-                dealt[:, :H].rearrange("p (t c i) -> p c t i", t=4, i=16),
-                got[:, :H].rearrange("p (c i t) -> p c t i", t=4, i=16),
-            )
-            nc.vector.tensor_copy(dealt[:, H:].bitcast(I32), got[:, H:].bitcast(I32))
-            plane = dealt
-            for i in range(1, 4):
-                nc.sync.dma_start(plane[i:P:32, :].bitcast(I32), dealt[8 * i:P:32, :].bitcast(I32))
+        def coded_layer(code_list, token_list, name):
+            dealt = keep.tile([P, H], U8, name=name + "_dealt", align_bytes=64)
+
+            def deal_bytes(got):
+                nc.vector.tensor_copy(
+                    dealt[:].rearrange("p (t c i) -> p c t i", t=4, i=16),
+                    got[:].rearrange("p (c i t) -> p c t i", t=4, i=16),
+                )
+                for i in range(1, 4):
+                    nc.sync.dma_start(dealt[i:P:32, :].bitcast(I32), dealt[8 * i:P:32, :].bitcast(I32))
+
             if name == "b":
+                got = keep.tile([P, H], U8, name="b_got")
+                nc.vector.tensor_copy(got[:], d_bytes[:].indirect(code_list[:]))
+                deal_bytes(got)
                 xq = keep.tile([P, S], U32, name="b_xq", align_bytes=64)
                 nc.vector.tensor_copy(xq[:], x_tab[:].indirect(token_list[:]))
-                dq = keep.tile([P, H], U32, name="b_dq", tag="chain", align_bytes=64)
+                x_plane = keep.tile([P, S], U8, name="b_x_plane", align_bytes=64)
+                nc.vector.tensor_copy(x_plane[:], x_bytes[:].indirect(token_list[:]))
+                dq = relay.tile([P, H], U32, name="b_dq", offset=3584, align_bytes=64)
                 nc.vector.tensor_copy(dq[:], d_tab[:].indirect(code_list[:]))
             else:
-                both = keep.tile([P, H + S], U32, name="a_words", tag="chain", align_bytes=64)
+                got = relay.tile([P, H], U8, name="a_got", offset=3584, align_bytes=64)
+                nc.vector.tensor_copy(got[:], d_bytes[:].indirect(code_list[:]))
+                x_plane = relay.tile([P, S], U8, name="a_x_plane", offset=4096, align_bytes=64)
+                nc.vector.tensor_copy(x_plane[:], x_bytes[:].indirect(token_list[:]))
+                deal_bytes(got)
+                both = relay.tile([P, H + S], U32, name="a_words", offset=0, align_bytes=64)
                 dq, xq = both[:, :H], both[:, H:]
                 nc.vector.tensor_copy(dq, d_tab[:].indirect(code_list[:]))
                 nc.vector.tensor_copy(xq, x_tab[:].indirect(token_list[:]))
@@ -109,8 +118,8 @@ def tile_picked_twpqpullbnorm2_none_p_kernel(
                 acc = psum.tile([P, S], F32, name="%s_acc%d" % (name, t), tag="bank_%s%d" % (name, t))
                 cols = slice(t * P, (t + 1) * P)
                 nc.tensor.matmul_mx(
-                    acc[:], lhsT=dd[:, cols].bitcast(FP8X4), lhsT_scale=plane[:, cols],
-                    rhs=xq[:].bitcast(FP8X4), rhs_scale=plane[:, H:], start=True, stop=True,
+                    acc[:], lhsT=dd[:, cols].bitcast(FP8X4), lhsT_scale=dealt[:, cols],
+                    rhs=xq[:].bitcast(FP8X4), rhs_scale=x_plane[:], start=True, stop=True,
                 )
                 banks.append(acc)
             return banks
@@ -130,23 +139,21 @@ def tile_picked_twpqpullbnorm2_none_p_kernel(
             cols = slice(c * 256, (c + 1) * 256)
             nc.vector.quantize_mx(w_codes[:, cols].bitcast(FP8X4), w_plane[:, cols], w_bf[c][:].rearrange("p n t -> p (n t)"))
 
+        b_acc = coded_layer(k2_t, two_t, "b")
+        n1_t = load_list(n1, "n1_t")
         round_w(0, "w_bf0")
-        b_acc = coded_layer(k2_t, two_t, "b", ("b_got", "b_xq", "chain", "b_dealt"))
         n4_t = load_list(n4, "n4_t")
         n3_t = load_list(n3, "n3_t")
         load_w(1)
-        a_acc = coded_layer(k1_t, offs_t, "a", ("chain", "chain", "a_dq", "a_dealt"))
+        a_acc = coded_layer(k1_t, offs_t, "a")
 
         db = [keep.tile([P, S], F32, name="db%d" % t, tag="db%d" % t, align_bytes=64) for t in range(4)]
         other = [keep.tile([P, S], F32, name="bo%d" % t) for t in range(4)]
         for t in range(4):
             nc.scalar.copy(b_win[t][:, :S], b_acc[t][:])
-            if t > 0:
-                nc.scalar.activation(other[t][:], b_win[t][:].indirect(n2_t[:]), ACT.Copy)
-        nc.vector.tensor_scalar(other[0][:], b_win[0][:, :S], -1.0, None, ALU.mult)
+            nc.scalar.activation(other[t][:], b_win[t][:].indirect(n2_t[:]), ACT.Copy)
         quantize_w(0)
-        nc.vector.tensor_tensor(db[0][:], b_win[0][:].indirect(n2_t[:]), other[0][:], ALU.add)
-        for t in range(1, 4):
+        for t in range(4):
             nc.vector.tensor_tensor(db[t][:], other[t][:], b_acc[t][:], ALU.subtract)
 
         a_neg = keep.tile([P, 4, S], F32, name="a_neg")
@@ -203,7 +210,8 @@ def tile_picked_twpqpullbnorm2_none_p_kernel(
                 row.append(acc)
             h_acc.append(row)
 
-        leave_bank(0)
+        nc.scalar.activation(a_neg[:, 0, :], a_acc[0][:], ACT.Copy, scale=g_pos[0][:])
+        sg.append(keep.tile([P, S], F32, name="sg0", tag="gate0"))
         leave_bank(1)
         gate(0, whole)
         leave_bank(2)
@@ -220,6 +228,7 @@ def tile_picked_twpqpullbnorm2_none_p_kernel(
         round_w(1, "db3")
         nc.scalar.activation(warm[:, 2, :], sg[3][:, S - 8:], ACT.Abs_reciprocal_sqrt, bias=0.5)
 
+        nc.vector.tensor_scalar(a_win[0][:, :S], a_neg[:, 0, :], -1.0, None, ALU.mult)
         diff(0, whole)
         diff(1, whole)
         weigh(0, whole)

from contextlib import ExitStack

import concourse.mybir as mybir

F32 = mybir.dt.float32
BF16 = mybir.dt.bfloat16
I32 = mybir.dt.int32
U32 = mybir.dt.uint32
U16 = mybir.dt.uint16
U8 = mybir.dt.uint8
FP8X4 = mybir.dt.float8_e4m3fn_x4
ALU = mybir.AluOpType
ACT = mybir.ActivationFunctionType

P = 128
K, T, S, N, G, H = 512, 1024, 512, 512, 2048, 512
SPARE = 16
HALF = S // 2
FLOPS = 3 * 2 * 512 * 512 * 512

B_ON_VECTOR = [0]
SPLIT = [2,3]
MAG_ON_VECTOR = []


def tile_picked_twpqpullbnorm2_none_p_kernel(
    tc, x_words, x_scales, d_words, d_scales, gn, w1, offs, k1, two, k2, n1, n2, n3, n4, out
):
    nc = tc.nc
    with ExitStack() as ctx:
        lists = ctx.enter_context(tc.tile_pool(name="lists", bufs=1))
        keep = ctx.enter_context(tc.tile_pool(name="keep", bufs=1))
        relay = ctx.enter_context(tc.tile_pool(name="relay", bufs=1))
        psum = ctx.enter_context(tc.psum_pool(name="psum", bufs=1))

        def load_list(src, name):
            t = lists.tile([P, S // 16], U16, name=name)
            nc.sync.dma_start(t[:], src)
            return t

        warm = keep.tile([P, 3, 8], F32, name="warm")
        d_bytes = keep.tile([P, G], U8, name="d_bytes")
        x_bytes = keep.tile([P, T], U8, name="x_bytes")
        nc.gpsimd.memset(d_bytes[:].bitcast(I32), 0)
        nc.vector.memset(x_bytes[:].bitcast(I32), 0)
        nc.sync.dma_start(d_bytes[0:P:8, :].bitcast(I32), d_scales[0].bitcast(I32))
        k2_t = load_list(k2, "k2_t")
        two_t = load_list(two, "two_t")
        x_tab = keep.tile([P, T], U32, name="x_tab")
        nc.sync.dma_start(x_tab[:].bitcast(I32), x_words[0].rearrange("p n t -> p (n t)").bitcast(I32))
        for i in range(4):
            nc.sync.dma_start(x_bytes[i:P:32, :].bitcast(I32), x_scales[0, i:16:4, :].bitcast(I32))
        d_tab = keep.tile([P, G], U32, name="d_tab")
        nc.sync.dma_start(d_tab[:].bitcast(I32), d_words[0].rearrange("p n t -> p (n t)").bitcast(I32))
        k1_t = load_list(k1, "k1_t")
        offs_t = load_list(offs, "offs_t")
        w_raw = [keep.tile([P, 4, N // 2], F32, name="w_raw%d" % c) for c in range(2)]

        def load_w(c):
            nc.sync.dma_start(w_raw[c][:], w1[:, c * 256:(c + 1) * 256].rearrange("(p j) n -> p j n", j=4))

        n2_t = load_list(n2, "n2_t")
        load_w(0)
        gain = keep.tile([P, 4], F32, name="gain")
        nc.gpsimd.dma_start(gain[:], gn.rearrange("(p t) o -> p (t o)", t=4))
        nc.vector.memset(warm[:, 0, :], 1.0)
        nc.scalar.activation(warm[:, 1, :], warm[:, 0, :], ACT.Sigmoid)
        b_win = [keep.tile([P, S + SPARE], F32, name="b_win%d" % t) for t in range(4)]
        a_win = [keep.tile([P, S + SPARE], F32, name="a_win%d" % t) for t in range(3)]
        h_win = [keep.tile([P, S + SPARE], F32, name="h_win%d" % t) for t in range(4)]
        m_win = [keep.tile([P, S + SPARE], F32, name="m_win%d" % t) for t in range(4)]
        for t in b_win + a_win + h_win + m_win:
            nc.gpsimd.memset(t[:, S:], 0.0)
        g_pos = [keep.tile([P, 1], F32, name="g_pos%d" % t, tag="gate%d" % t) for t in range(4)]
        g_neg = keep.tile([P, 4], F32, name="g_neg")
        for t in range(4):
            nc.gpsimd.tensor_scalar(g_pos[t][:], gain[:, t:t + 1], 0.0625 if t in (1, 2) else -0.0625, 0.0, ALU.mult, ALU.add)
        nc.gpsimd.tensor_scalar(g_neg[:], gain[:], -0.0625, 0.0, ALU.mult, ALU.add)

        def coded_layer(code_list, token_list, name):
            dealt = keep.tile([P, H], U8, name=name + "_dealt", align_bytes=64)

            def deal_bytes(got):
                nc.vector.tensor_copy(
                    dealt[:].rearrange("p (t c i) -> p c t i", t=4, i=16),
                    got[:].rearrange("p (c i t) -> p c t i", t=4, i=16),
                )
                for i in range(1, 4):
                    nc.sync.dma_start(dealt[i:P:32, :].bitcast(I32), dealt[8 * i:P:32, :].bitcast(I32))

            if name == "b":
                got = keep.tile([P, H], U8, name="b_got")
                nc.vector.tensor_copy(got[:], d_bytes[:].indirect(code_list[:]))
                deal_bytes(got)
                xq = keep.tile([P, S], U32, name="b_xq", align_bytes=64)
                nc.vector.tensor_copy(xq[:], x_tab[:].indirect(token_list[:]))
                x_plane = keep.tile([P, S], U8, name="b_x_plane", align_bytes=64)
                nc.vector.tensor_copy(x_plane[:], x_bytes[:].indirect(token_list[:]))
                dq = relay.tile([P, H], U32, name="b_dq", offset=3584, align_bytes=64)
                nc.vector.tensor_copy(dq[:], d_tab[:].indirect(code_list[:]))
            else:
                got = relay.tile([P, H], U8, name="a_got", offset=3584, align_bytes=64)
                nc.vector.tensor_copy(got[:], d_bytes[:].indirect(code_list[:]))
                x_plane = relay.tile([P, S], U8, name="a_x_plane", offset=4096, align_bytes=64)
                nc.vector.tensor_copy(x_plane[:], x_bytes[:].indirect(token_list[:]))
                deal_bytes(got)
                both = relay.tile([P, H + S], U32, name="a_words", offset=0, align_bytes=64)
                dq, xq = both[:, :H], both[:, H:]
                nc.vector.tensor_copy(dq, d_tab[:].indirect(code_list[:]))
                nc.vector.tensor_copy(xq, x_tab[:].indirect(token_list[:]))
            dd = keep.tile([P, H], U32, name=name + "_dd", align_bytes=64)
            nc.vector.tensor_copy(
                dd[:].rearrange("p (t c i) -> p c t i", t=4, i=4),
                dq[:].rearrange("p (c i t) -> p c t i", t=4, i=4),
            )
            banks = []
            for t in range(4):
                acc = psum.tile([P, S], F32, name="%s_acc%d" % (name, t), tag="bank_%s%d" % (name, t))
                cols = slice(t * P, (t + 1) * P)
                nc.tensor.matmul_mx(
                    acc[:], lhsT=dd[:, cols].bitcast(FP8X4), lhsT_scale=dealt[:, cols],
                    rhs=xq[:].bitcast(FP8X4), rhs_scale=x_plane[:], start=True, stop=True,
                )
                banks.append(acc)
            return banks

        w_codes = keep.tile([P, N], U32, name="w_codes", align_bytes=64)
        w_plane = keep.tile([P, N], U8, name="w_plane", align_bytes=64)
        w_bf = []

        def round_w(c, tag):
            w_bf.append(keep.tile([P, N // 2, 4], BF16, name="w_bf%d" % c, tag=tag, align_bytes=64))
            nc.scalar.copy(
                w_bf[c][:].rearrange("p (c i) t -> p c t i", i=2),
                w_raw[c][:].rearrange("p t (c i) -> p c t i", i=2),
            )

        def quantize_w(c):
            cols = slice(c * 256, (c + 1) * 256)
            nc.vector.quantize_mx(w_codes[:, cols].bitcast(FP8X4), w_plane[:, cols], w_bf[c][:].rearrange("p n t -> p (n t)"))

        b_acc = coded_layer(k2_t, two_t, "b")
        n1_t = load_list(n1, "n1_t")
        round_w(0, "w_bf0")
        n4_t = load_list(n4, "n4_t")
        n3_t = load_list(n3, "n3_t")
        load_w(1)
        a_acc = coded_layer(k1_t, offs_t, "a")

        db = [keep.tile([P, S], F32, name="db%d" % t, tag="db%d" % t, align_bytes=64) for t in range(4)]
        other = [keep.tile([P, S], F32, name="bo%d" % t) for t in range(4)]
        for t in range(4):
            nc.scalar.copy(b_win[t][:, :S], b_acc[t][:])
            nc.scalar.activation(other[t][:], b_win[t][:].indirect(n2_t[:]), ACT.Copy)
        quantize_w(0)
        for t in range(4):
            nc.vector.tensor_tensor(db[t][:], other[t][:], b_acc[t][:], ALU.subtract)

        a_neg = keep.tile([P, 4, S], F32, name="a_neg")
        pull = keep.tile([P, 4, S], F32, name="pull")
        da = [keep.tile([P, S], F32, name="da%d" % t) for t in range(4)]
        sg = []
        whole, first, second = (0, S), (0, HALF), (HALF, S)

        def leave_bank(t):
            nc.scalar.activation(a_neg[:, t, :], a_acc[t][:], ACT.Copy, scale=g_neg[:, t:t + 1])
            nc.scalar.activation(a_win[t][:, :S], a_acc[t][:], ACT.Copy, scale=g_pos[t][:])
            sg.append(keep.tile([P, S], F32, name="sg%d" % t, tag="gate%d" % t))

        def gate(t, span):
            lo, hi = span
            nc.scalar.activation(sg[t][:, lo:hi], db[t][:, lo:hi], ACT.Sigmoid, scale=0.0625)

        def diff(t, span):
            lo, hi = span
            if t == 3:
                nc.vector.scalar_tensor_tensor(da[t][:, lo:hi], a_acc[t][:, lo:hi], g_neg[:, t:t + 1], fetched[:, lo:hi], ALU.mult, ALU.subtract)
                return
            nc.vector.tensor_tensor(da[t][:, lo:hi], a_win[t][:].indirect(n1_t[:, lo // 16:hi // 16]), a_neg[:, t, lo:hi], ALU.add)

        def weigh(t, span):
            lo, hi = span
            nc.vector.tensor_tensor(pull[:, t, lo:hi], sg[t][:, lo:hi], da[t][:, lo:hi], ALU.mult)

        z_codes = keep.tile([P, S], U32, name="z_codes", align_bytes=64)
        z_plane = keep.tile([P, S], U8, name="z_plane", align_bytes=64)
        z_bf = [keep.tile([P, HALF, 4], BF16, name="z_bf%d" % c, align_bytes=64) for c in range(2)]
        h_acc = []

        def blend(c):
            cols = slice(c * HALF, (c + 1) * HALF)
            nc.vector.tensor_tensor(
                z_bf[c][:].rearrange("p (c i) t -> p c t i", i=2),
                pull[:, :, cols].rearrange("p t (c i) -> p c t i", i=2),
                a_neg[:, :, cols].rearrange("p t (c i) -> p c t i", i=2),
                ALU.subtract,
            )

        def dense(c):
            cols = slice(c * HALF, (c + 1) * HALF)
            nc.vector.quantize_mx(z_codes[:, cols].bitcast(FP8X4), z_plane[:, cols], z_bf[c][:].rearrange("p n t -> p (n t)"))
            row = []
            for t in range(4):
                acc = psum.tile([P, HALF], F32, name="h_acc%d%d" % (c, t), tag="bank_%s%d" % ("ba"[c], t))
                rows = slice(t * P, (t + 1) * P)
                nc.tensor.matmul_mx(
                    acc[:], lhsT=w_codes[:, rows].bitcast(FP8X4), lhsT_scale=w_plane[:, rows],
                    rhs=z_codes[:, cols].bitcast(FP8X4), rhs_scale=z_plane[:, cols], start=True, stop=True,
                )
                row.append(acc)
            h_acc.append(row)

        nc.scalar.activation(a_neg[:, 0, :], a_acc[0][:], ACT.Copy, scale=g_pos[0][:])
        sg.append(keep.tile([P, S], F32, name="sg0", tag="gate0"))
        leave_bank(1)
        gate(0, whole)
        leave_bank(2)
        gate(1, whole)
        nc.scalar.activation(a_neg[:, 3, :], a_acc[3][:], ACT.Copy, scale=g_pos[3][:])
        sg.append(keep.tile([P, S], F32, name="sg3", tag="gate3"))
        fetched = keep.tile([P, S], F32, name="fetched")
        nc.scalar.activation(fetched[:, :HALF], a_neg[:, 3, :].indirect(n1_t[:, :16]), ACT.Copy)
        gate(2, first)
        gate(3, first)
        nc.scalar.activation(fetched[:, HALF:], a_neg[:, 3, :].indirect(n1_t[:, 16:]), ACT.Copy)
        gate(2, second)
        gate(3, second)
        round_w(1, "db3")
        nc.scalar.activation(warm[:, 2, :], sg[3][:, S - 8:], ACT.Abs_reciprocal_sqrt, bias=0.5)

        nc.vector.tensor_scalar(a_win[0][:, :S], a_neg[:, 0, :], -1.0, None, ALU.mult)
        diff(0, whole)
        diff(1, whole)
        weigh(0, whole)
        diff(2, first)
        weigh(1, whole)
        diff(3, first)
        weigh(2, first)
        weigh(3, first)
        diff(2, second)
        blend(0)
        diff(3, second)
        quantize_w(1)
        dense(0)
        weigh(2, second)
        weigh(3, second)
        blend(1)
        mag = [keep.tile([P, S], F32, name="mag%d" % t) for t in range(4)]
        for t in range(4):
            nc.scalar.activation(m_win[t][:, :HALF], h_acc[0][t][:], ACT.Abs)
            nc.vector.tensor_copy(mag[t][:, :HALF], m_win[t][:, :HALF])
            if t == 0:
                dense(1)
        for t in range(4):
            nc.scalar.activation(m_win[t][:, HALF:S], h_acc[1][t][:], ACT.Abs)
            if t in MAG_ON_VECTOR:
                nc.vector.tensor_copy(mag[t][:, HALF:], m_win[t][:, HALF:S])
            else:
                nc.scalar.activation(mag[t][:, HALF:], h_acc[1][t][:], ACT.Abs)
        den = [keep.tile([P, S], F32, name="den%d" % t) for t in range(4)]
        for t in range(4):
            nc.vector.tensor_tensor(den[t][:], m_win[t][:].indirect(n4_t[:]), mag[t][:], ALU.add)
        for t in range(4):
            nc.scalar.copy(h_win[t][:, :HALF], h_acc[0][t][:])
        r = []
        for t in range(4):
            q = keep.tile([P, S], F32, name="q%d" % t)
            nc.scalar.activation(q[:], den[t][:], ACT.Abs_reciprocal_sqrt, bias=0.5)
            r.append(keep.tile([P, S], F32, name="r%d" % t))
            nc.scalar.activation(r[t][:], q[:], ACT.Square)
            nc.scalar.copy(h_win[t][:, HALF:S], h_acc[1][t][:])
        for t in range(4):
            o = keep.tile([P, S], F32, name="o%d" % t)
            for lo, hi in ([(0, S)] if t < 3 else [(0, HALF), (HALF, S)]):
                nc.vector.tensor_tensor(o[:, lo:hi], h_win[t][:].indirect(n3_t[:, lo // 16:hi // 16]), r[t][:, lo:hi], ALU.mult)
                nc.sync.dma_start(out[t * P:(t + 1) * P, lo:hi], o[:, lo:hi])
